import numpy as np
import ml_dtypes


def mxq(x, axis, fmt="e4m3"):
    dtype, down = {"e4m3": (ml_dtypes.float8_e4m3fn, 7), "e5m2": (ml_dtypes.float8_e5m2, 14)}[fmt]
    v = np.moveaxis(np.asarray(x, np.float32).astype(ml_dtypes.bfloat16).astype(np.float64), axis, -1)
    blocks = v.reshape(v.shape[:-1] + (-1, 32))
    amax = np.abs(blocks).max(-1, keepdims=True)
    byte = np.maximum(np.where(amax > 0, np.frexp(amax)[1] - 1 + 127, 0) - down, 1)
    scale = np.exp2(byte - 127.0)
    codes = (blocks / scale).astype(np.float32).astype(dtype).astype(np.float64)
    return np.moveaxis((codes * scale).reshape(v.shape), -1, axis)


WIDE = False


def mx_kscale(k):
    if not WIDE:
        return np.ones(k)
    levels = np.array([10, -10, 5, -5, 0])
    if k % 512:
        return np.exp2(np.random.permutation(np.resize(levels, k // 32))).repeat(32)
    a = np.empty((k // 512, 16))
    for p in range(k // 512):
        a[p, :8] = np.random.permutation(np.resize(levels, 8))
        for g in range(8):
            far = levels[np.abs(levels - a[p, g]) >= 10]
            a[p, g + 8] = far[np.random.randint(len(far))]
    return np.exp2(a.ravel()).repeat(32)


BF16 = ml_dtypes.bfloat16


def bf(x):
    return np.asarray(x, np.float32).astype(BF16)


def f64(x):
    return np.asarray(x).astype(np.float64)


E2M1 = np.array([0.0, 0.5, 1.0, 1.5, 2.0, 3.0, 4.0, 6.0, -0.0, -0.5, -1.0, -1.5, -2.0, -3.0, -4.0, -6.0])


def pack_weight(w, fmt):
    k, n = w.shape
    w = f64(bf(w)).reshape(k // 32, 32, n)
    amax = np.abs(w).max(1)
    if fmt == "e4m3":
        byte = np.frexp(amax)[1] - 1 + 127 - 7
    else:
        mant, ex = np.frexp(amax / 6.0)
        byte = np.where(mant > 0.5, ex, ex - 1) + 127
    byte = np.clip(np.where(amax > 0, byte, 1), 1, 254)
    scaled = (w * np.exp2(127.0 - byte)[:, None, :]).reshape(k, n).astype(np.float32)
    by_word = np.ascontiguousarray(scaled.reshape(k // 512, 128, 4, n).transpose(0, 1, 3, 2))
    if fmt == "e4m3":
        words = by_word.astype(ml_dtypes.float8_e4m3fn).view(np.uint8)
    else:
        c = by_word.astype(ml_dtypes.float4_e2m1fn).view(np.uint8) & 0xF
        words = c[..., 0::2] | (c[..., 1::2] << 4)
    return np.ascontiguousarray(words), np.ascontiguousarray(byte.astype(np.uint8).reshape(k // 512, 16, n))


def unpack_weight(words, scales, fmt):
    g, p, n, _ = words.shape
    if fmt == "e4m3":
        vals = np.ascontiguousarray(words).view(ml_dtypes.float8_e4m3fn).astype(np.float64)
    else:
        nib = np.empty((g, p, n, 4), np.uint8)
        nib[..., 0::2] = words & 0xF
        nib[..., 1::2] = words >> 4
        vals = E2M1[nib]
    vals = vals * np.repeat(np.exp2(scales.astype(np.float64) - 127.0), 8, axis=1)[..., None]
    return vals.transpose(0, 1, 3, 2).reshape(g * 512, n)
def pack4(w):
    words, scales = pack_weight(w, "e2m1")
    return words.reshape(words.shape[0], 128, -1), scales


def unpack4(words, scales):
    return unpack_weight(words.reshape(words.shape[0], 128, -1, 2), scales, "e2m1")


E4M3FN = np.array([(-1.0 if i & 128 else 1.0) * ((1.0 + (i & 7) / 8.0) * 2.0 ** (((i >> 3) & 15) - 7) if i & 120 else (i & 7) * 2.0 ** -9) for i in range(256)])


def e4m3fn_bytes(y):
    return np.clip(np.asarray(y, np.float64), -448.0, 448.0).astype(np.float32).astype(ml_dtypes.float8_e4m3fn).view(np.uint8)


def e4m3fn_values(b):
    return E4M3FN[b]


B, S, D1, D2, C1, C2 = 2, 1024, 512, 1024, 1024, 512


def leaky(z):
    return np.where(z > 0, z, 0.2 * z)


def draw0():
    s1, s2 = mx_kscale(D1), mx_kscale(D2)
    u = mx_kscale(S)
    x1 = np.random.standard_normal((B, S, D1)) * s1
    x2 = np.random.standard_normal((B, S, D2)) * s2 / u[:, None]
    w1 = np.random.standard_normal((D1, C1)) * (1.4 / np.sqrt(D1)) / s1[:, None]
    w2 = np.random.standard_normal((D2, C2)) * (1.4 / np.sqrt(D2)) / s2[:, None]
    m = np.random.standard_normal((B, S)) * u
    a = np.random.standard_normal((B, C1, C2)) * 0.5
    w1_words, w1_scales = pack4(w1)
    w2_words, w2_scales = pack4(w2)
    return {"x1": bf(x1), "x2": bf(x2), "w1_words": w1_words, "w1_scales": w1_scales, "w2_words": w2_words, "w2_scales": w2_scales, "m": bf(m), "a": bf(a)}


def core(x1, x2, w1_words, w1_scales, w2_words, w2_scales, m, a):
    z1 = mxq(f64(x1), 2, "e4m3") @ unpack4(w1_words, w1_scales)
    z2 = mxq(f64(x2), 2, "e4m3") @ unpack4(w2_words, w2_scales)
    f1 = leaky(z1)
    f2 = leaky(z2)
    fm = f1 * f64(m)[:, :, None]
    gram = (mxq(fm, 1, "e4m3").transpose(0, 2, 1) @ mxq(f2, 1, "e4m3")) / np.sqrt(S)
    return np.tanh(gram - f64(a))


def setup_inputs():
    drawn = draw0()
    full = np.asarray(drawn['x1']).astype(np.float64)
    scale = (np.abs(full).reshape(2, 1024, 4, 128).max(axis=(3,)) / 448.0).astype(np.float32)
    given = {}
    for key, value in drawn.items():
        if key == 'x1':
            given['x1_bytes'] = e4m3fn_bytes(full / np.repeat(scale.astype(np.float64), 128, axis=2))
            given['x1_scale'] = scale
        else:
            given[key] = value
    return given


def reference(x1_bytes, x1_scale, x2, w1_words, w1_scales, w2_words, w2_scales, m, a):
    return core(e4m3fn_values(x1_bytes) * np.repeat(x1_scale.astype(np.float64), 128, axis=2), x2, w1_words, w1_scales, w2_words, w2_scales, m, a)

@@ -1,0 +1,262 @@
+from contextlib import ExitStack
+
+import concourse.mybir as mybir
+from concourse.masks import make_identity
+
+F32 = mybir.dt.float32
+BF16 = mybir.dt.bfloat16
+I32 = mybir.dt.int32
+U32 = mybir.dt.uint32
+U8 = mybir.dt.uint8
+FP8 = mybir.dt.float8_e4m3fn
+FP8X4 = mybir.dt.float8_e4m3fn_x4
+FP4X4 = mybir.dt.float4_e2m1fn_x4
+ALU = mybir.AluOpType
+ACT = mybir.ActivationFunctionType
+
+B, S, D1, D2, C1, C2 = 2, 1024, 512, 1024, 1024, 512
+FLOPS = 2 * B * S * (D1 * C1 + D2 * C2 + C1 * C2)
+
+P = 128
+T = 4
+KP = P * T
+NB = 512
+UNITS = B * S // KP
+G = S // KP
+SLOPE = 0.2
+
+
+def tile_crosslayerguidedstylegramlogcoshgrad_d1p_kernel(
+    tc, x1_bytes, x1_scale, x2, w1_words, w1_scales, w2_words, w2_scales, m, a, out
+):
+    nc = tc.nc
+    with ExitStack() as ctx:
+        keep = ctx.enter_context(tc.tile_pool(name="keep", bufs=1))
+        load = ctx.enter_context(tc.tile_pool(name="load", bufs=UNITS))
+        work = ctx.enter_context(tc.tile_pool(name="work", bufs=3))
+        code = ctx.enter_context(tc.tile_pool(name="code", bufs=2))
+        tr_psum = ctx.enter_context(tc.psum_pool(name="tr_psum", bufs=2))
+        z_psum = ctx.enter_context(tc.psum_pool(name="z_psum", bufs=4))
+        g_psum = ctx.enter_context(tc.psum_pool(name="g_psum", bufs=2))
+
+        ident = keep.tile([P, P], F32)
+        warm = keep.tile([P, 1], F32)
+        zero = keep.tile([P, 1], F32)
+        x1s = keep.tile([P, UNITS, T, 4], F32)
+        m_sb = keep.tile([P, UNITS, T], BF16)
+        sgn2 = keep.tile([P, UNITS, T], F32)
+        sgn = keep.tile([P, UNITS, T], BF16)
+        absm = keep.tile([P, UNITS, T], F32)
+        w1c = keep.tile([P, 2 * C1], U8, align_bytes=64)
+        w1p = keep.tile([P, C1], U8, align_bytes=64)
+        w2c = keep.tile([P, 2, 2 * C2], U8, align_bytes=64)
+        w2p = keep.tile([P, 2, C2], U8, align_bytes=64)
+        a_sb = keep.tile([P, B, C1 // P, C2], BF16)
+        f1c = keep.tile([P, B, G, C1], U32, align_bytes=64)
+        f1p = keep.tile([P, B, G, C1], U8, align_bytes=64)
+        f2c = keep.tile([P, B, G, C2], U32, align_bytes=64)
+        f2p = keep.tile([P, B, G, C2], U8, align_bytes=64)
+
+        x1_in, x1_bf, x2_in = {}, {}, {}
+        codes, planes, y, f, o_tiles = {}, {}, {}, {}, {}
+
+        def unit_rows(src, u):
+            return src[u // G, (u % G) * KP : (u % G + 1) * KP].rearrange("(p t) k -> p t k", t=T)
+
+        def load_x1(u):
+            x1_in[u] = load.tile([P, T, D1], U8, name="x1_in")
+            nc.sync.dma_start(out=x1_in[u][:], in_=unit_rows(x1_bytes, u))
+
+        def load_x2(u):
+            x2_in[u] = load.tile([P, T, D2], BF16, name="x2_in")
+            for h in range(2):
+                k = slice(h * KP, (h + 1) * KP)
+                nc.sync.dma_start(out=x2_in[u][:, :, k], in_=unit_rows(x2, u)[:, :, k])
+
+        def widen(u, pieces):
+            if u not in x1_bf:
+                x1_bf[u] = work.tile([P, T, D1], BF16, name="x1_bf")
+            for t, j, on_vector in pieces:
+                cols = slice(P * j, P * (j + 1))
+                src = x1_in[u][:, t, cols].bitcast(FP8)
+                scale = x1s[:, u, t, j : j + 1]
+                if on_vector:
+                    nc.vector.tensor_scalar(out=x1_bf[u][:, t, cols], in0=src, scalar1=scale, scalar2=None, op0=ALU.mult)
+                else:
+                    nc.scalar.activation(out=x1_bf[u][:, t, cols], in_=src, func=ACT.Copy, scale=scale)
+
+        def turn(u, kind, vector_banks=()):
+            if kind == "x1":
+                words = x1_bf[u][:].rearrange("p t k -> p (t k)").bitcast(F32)
+                row, first = D1 // 2, 0
+            else:
+                words = x2_in[u][:].rearrange("p t k -> p (t k)").bitcast(F32)
+                row, first = D2 // 2, (KP // 2) * kind
+            grouped = work.tile([P, KP, T], BF16, name="x_grouped", align_bytes=64)
+            gw = grouped[:].rearrange("p c j -> p (c j)").bitcast(F32)
+            for pair in range(2):
+                bank = tr_psum.tile([P, 2, 2, P], F32, name="x_bank")
+                for i in range(2):
+                    for e in range(2):
+                        at = row * (2 * pair + i) + first + e
+                        nc.tensor.transpose(bank[:, i, e, :], words[:, at : at + KP // 2 - 1 : 2], ident[:])
+                dst = gw[:, KP * pair : KP * (pair + 1)].rearrange("p (i r e) -> p i r e", i=2, e=2)
+                src = bank[:].rearrange("p i e r -> p i r e")
+                if pair in vector_banks:
+                    nc.vector.tensor_copy(out=dst, in_=src)
+                else:
+                    nc.scalar.copy(out=dst, in_=src)
+            return grouped
+
+        def quantize_x(u, kind, grouped):
+            c = code.tile([P, KP], U32, name="c_%s" % kind, align_bytes=64)
+            s = code.tile([P, KP], U8, name="s_%s" % kind, align_bytes=64)
+            nc.vector.quantize_mx(out=c[:].bitcast(FP8X4), scales=s[:], in_=grouped[:].rearrange("p c j -> p (c j)"))
+            codes[u, kind], planes[u, kind] = c, s
+
+        def project(u, part):
+            yt = work.tile([P, T, NB], F32, name="y")
+            for t in range(T):
+                cols = slice(P * t, P * (t + 1))
+                bank = z_psum.tile([P, NB], F32, name="z_bank")
+                kinds = (0, 1) if part == "f2" else ("x1",)
+                for i, kind in enumerate(kinds):
+                    if part == "f2":
+                        words, plane = w2c[:, kind, :], w2p[:, kind, :]
+                    else:
+                        words = w1c[:, 2 * NB * part : 2 * NB * (part + 1)]
+                        plane = w1p[:, NB * part : NB * (part + 1)]
+                    nc.tensor.matmul_mx(
+                        out=bank[:],
+                        lhsT=codes[u, kind][:, cols].bitcast(FP8X4),
+                        lhsT_scale=planes[u, kind][:, cols],
+                        rhs=words.bitcast(FP4X4),
+                        rhs_scale=plane,
+                        start=(i == 0),
+                        stop=(i == len(kinds) - 1),
+                    )
+                if part == "f2":
+                    nc.scalar.copy(out=yt[:, t, :], in_=bank[:])
+                else:
+                    nc.scalar.activation(out=yt[:, t, :], in_=bank[:], func=ACT.Copy, scale=absm[:, u, t : t + 1])
+            y[u, part] = yt
+
+        def leaky(u, part):
+            src = y[u, part][:].rearrange("p t n -> p n t")
+            ft = work.tile([P, NB, T], BF16, name="f", align_bytes=64)
+            nc.vector.scalar_tensor_tensor(out=ft[:], in0=src, scalar=SLOPE, in1=src, op0=ALU.mult, op1=ALU.max)
+            f[u, part] = ft
+
+        def sign(u):
+            ft = work.tile([P, NB, T], BF16, name="f_signed", align_bytes=64)
+            nc.vector.tensor_tensor(
+                out=ft[:], in0=f[u, "f2"][:], in1=sgn[:, u, :].unsqueeze(1).to_broadcast([P, NB, T]), op=ALU.mult
+            )
+            f[u, "f2"] = ft
+
+        def quantize_f(u, part):
+            b, g = u // G, u % G
+            if part == "f2":
+                c, s = f2c[:, b, g, :], f2p[:, b, g, :]
+            else:
+                cols = slice(NB * part, NB * (part + 1))
+                c, s = f1c[:, b, g, cols], f1p[:, b, g, cols]
+            nc.vector.quantize_mx(out=c.bitcast(FP8X4), scales=s, in_=f[u, part][:].rearrange("p n t -> p (n t)"))
+
+        def gram(b, pair):
+            o = work.tile([P, 2, C2], F32, name="o")
+            o_tiles[b, pair] = o
+            for i in range(2):
+                ib = 2 * pair + i
+                bank = g_psum.tile([P, C2], F32, name="g_bank")
+                for g in range(G):
+                    cols = slice(P * ib, P * (ib + 1))
+                    nc.tensor.matmul_mx(
+                        out=bank[:],
+                        lhsT=f1c[:, b, g, cols].bitcast(FP8X4),
+                        lhsT_scale=f1p[:, b, g, cols],
+                        rhs=f2c[:, b, g, :].bitcast(FP8X4),
+                        rhs_scale=f2p[:, b, g, :],
+                        start=(g == 0),
+                        stop=(g == G - 1),
+                    )
+                nc.vector.scalar_tensor_tensor(
+                    out=o[:, i, :], in0=bank[:], scalar=1.0 / 32.0, in1=a_sb[:, b, ib, :], op0=ALU.mult, op1=ALU.subtract
+                )
+
+        def finish(b, pair, step=2):
+            o = o_tiles[b, pair]
+            rows = out[b, 2 * P * pair : 2 * P * (pair + 1)].rearrange("(i p) n -> p i n", p=P)
+            for i in range(0, 2, step):
+                nc.scalar.activation(out=o[:, i : i + step], in_=o[:, i : i + step], func=ACT.Tanh)
+                nc.sync.dma_start(out=rows[:, i : i + step], in_=o[:, i : i + step])
+
+        ctx.enter_context(tc.manual_schedule())
+        nc.vector.memset(zero[:], 0.0)
+        nc.vector.memset(w1p[:].bitcast(I32), 0)
+        nc.vector.memset(w2p[:].rearrange("p g n -> p (g n)").bitcast(I32), 0)
+        make_identity(nc, ident[:])
+        nc.gpsimd.dma_start(out=m_sb[:], in_=m.rearrange("b (g p t) -> p (b g) t", g=G, t=T))
+        load_x1(0)
+        nc.sync.dma_start(out=x1s[:].rearrange("p u t j -> p u (t j)"),
+                          in_=x1_scale.rearrange("b (g p t) j -> p (b g) (t j)", g=G, t=T))
+        load_x2(0)
+        nc.sync.dma_start(out=w1c[:].bitcast(I32), in_=w1_words[0].bitcast(I32))
+        for q in range(4):
+            nc.scalar.dma_start(out=w1p[32 * q : 32 * q + 4, :].bitcast(I32),
+                                in_=w1_scales[0, 4 * q : 4 * q + 4, :].bitcast(I32))
+        load_x1(1)
+        nc.sync.dma_start(out=w2c[:].bitcast(I32), in_=w2_words.rearrange("g p n -> p g n").bitcast(I32))
+        for q in range(4):
+            nc.gpsimd.dma_start(out=w2p[32 * q : 32 * q + 4, :, :].bitcast(I32),
+                                in_=w2_scales[:, 4 * q : 4 * q + 4, :].rearrange("g r n -> r g n").bitcast(I32))
+        nc.scalar.activation(out=warm[:], in_=zero[:], func=ACT.Tanh)
+        nc.gpsimd.tensor_scalar(out=sgn2[:], in0=m_sb[:], scalar1=0.0, scalar2=2.0, op0=ALU.is_ge, op1=ALU.mult)
+        nc.gpsimd.tensor_scalar(out=sgn[:], in0=sgn2[:], scalar1=1.0, scalar2=0.0, op0=ALU.subtract, op1=ALU.add)
+        nc.gpsimd.tensor_tensor(out=absm[:], in0=m_sb[:], in1=sgn[:], op=ALU.mult)
+        for u in range(1, UNITS):
+            if u > 1:
+                load_x1(u)
+            load_x2(u)
+        for b in range(B):
+            nc.sync.dma_start(out=a_sb[:, b], in_=a[b].rearrange("(i p) n -> p i n", p=P))
+
+        def pieces(v_count):
+            order = [(t, j) for t in range(T) for j in range(4)]
+            return [(t, j, (n * v_count) // 16 != ((n + 1) * v_count) // 16) for n, (t, j) in enumerate(order)]
+
+        chunks = [(0, 0), (0, 1), (0, "f2")]
+        turns = [(0, "x1"), (0, 0), (0, 1)]
+        for u in range(1, UNITS):
+            chunks += [(u, "f2"), (u, 0), (u, 1)]
+            turns += [(u, 0), (u, 1), (u, "x1")]
+        grams = {6: [(0, 0)], 7: [(0, 1)], 8: [(0, 2)], 9: [(0, 3)], 11: [(1, 0)]}
+
+        widen(0, pieces(10))
+        for item in turns[:2]:
+            quantize_x(*item, turn(*item, vector_banks=(1,)))
+        widen(1, pieces(5)[0::3])
+        turned = []
+        for k, (u, part) in enumerate(chunks):
+            for item in turned:
+                quantize_x(*item)
+            if k > 0:
+                quantize_f(*chunks[k - 1])
+            project(u, part)
+            for pair in grams.get(k - 1, ()):
+                finish(*pair)
+            for pair in grams.get(k, ()):
+                gram(*pair)
+            turned = [item + (turn(*item, vector_banks=()),) for item in (turns[2:4] if k == 0 else turns[k + 3 : k + 4])]
+            nxt = (k + 1) // 3 + 1
+            if nxt < UNITS:
+                widen(nxt, pieces(5)[(k + 1) % 3 :: 3])
+            leaky(u, part)
+            if part == "f2":
+                sign(u)
+        quantize_f(*chunks[-1])
+        for pair in grams[11]:
+            finish(*pair)
+        for pair in range(4 - len(grams[11])):
+            gram(1, len(grams[11]) + pair)
+            finish(1, len(grams[11]) + pair, 1)

@@ -67,9 +67,10 @@ def tile_crosslayerguidedstylegramlogcoshgrad_d1p_kernel(
             x1_in[u] = load.tile([P, T, D1], U8, name="x1_in")
             nc.sync.dma_start(out=x1_in[u][:], in_=unit_rows(x1_bytes, u))
 
-        def load_x2(u):
-            x2_in[u] = load.tile([P, T, D2], BF16, name="x2_in")
-            for h in range(2):
+        def load_x2(u, halves=(0, 1)):
+            if u not in x2_in:
+                x2_in[u] = load.tile([P, T, D2], BF16, name="x2_in")
+            for h in halves:
                 k = slice(h * KP, (h + 1) * KP)
                 nc.sync.dma_start(out=x2_in[u][:, :, k], in_=unit_rows(x2, u)[:, :, k])
 
@@ -196,20 +197,21 @@ def tile_crosslayerguidedstylegramlogcoshgrad_d1p_kernel(
         nc.vector.memset(w1p[:].bitcast(I32), 0)
         nc.vector.memset(w2p[:].rearrange("p g n -> p (g n)").bitcast(I32), 0)
         make_identity(nc, ident[:])
-        nc.gpsimd.dma_start(out=m_sb[:], in_=m.rearrange("b (g p t) -> p (b g) t", g=G, t=T))
         load_x1(0)
         nc.sync.dma_start(out=x1s[:].rearrange("p u t j -> p u (t j)"),
                           in_=x1_scale.rearrange("b (g p t) j -> p (b g) (t j)", g=G, t=T))
-        load_x2(0)
+        load_x2(0, (0,))
+        nc.sync.dma_start(out=m_sb[:], in_=m.rearrange("b (g p t) -> p (b g) t", g=G, t=T))
+        for q in range(4):
+            nc.sync.dma_start(out=w1p[32 * q : 32 * q + 4, :].bitcast(I32),
+                              in_=w1_scales[0, 4 * q : 4 * q + 4, :].bitcast(I32))
         nc.sync.dma_start(out=w1c[:].bitcast(I32), in_=w1_words[0].bitcast(I32))
-        for q in range(4):
-            nc.scalar.dma_start(out=w1p[32 * q : 32 * q + 4, :].bitcast(I32),
-                                in_=w1_scales[0, 4 * q : 4 * q + 4, :].bitcast(I32))
+        load_x2(0, (1,))
         load_x1(1)
-        nc.sync.dma_start(out=w2c[:].bitcast(I32), in_=w2_words.rearrange("g p n -> p g n").bitcast(I32))
         for q in range(4):
-            nc.gpsimd.dma_start(out=w2p[32 * q : 32 * q + 4, :, :].bitcast(I32),
-                                in_=w2_scales[:, 4 * q : 4 * q + 4, :].rearrange("g r n -> r g n").bitcast(I32))
+            nc.sync.dma_start(out=w2p[32 * q : 32 * q + 4, :, :].bitcast(I32),
+                              in_=w2_scales[:, 4 * q : 4 * q + 4, :].rearrange("g r n -> r g n").bitcast(I32))
+        nc.sync.dma_start(out=w2c[:].bitcast(I32), in_=w2_words.rearrange("g p n -> p g n").bitcast(I32))
         nc.scalar.activation(out=warm[:], in_=zero[:], func=ACT.Tanh)
         nc.gpsimd.tensor_scalar(out=sgn2[:], in0=m_sb[:], scalar1=0.0, scalar2=2.0, op0=ALU.is_ge, op1=ALU.mult)
         nc.gpsimd.tensor_scalar(out=sgn[:], in0=sgn2[:], scalar1=1.0, scalar2=0.0, op0=ALU.subtract, op1=ALU.add)
@@ -232,10 +234,12 @@ def tile_crosslayerguidedstylegramlogcoshgrad_d1p_kernel(
             turns += [(u, 0), (u, 1), (u, "x1")]
         grams = {6: [(0, 0)], 7: [(0, 1)], 8: [(0, 2)], 9: [(0, 3)], 11: [(1, 0)]}
 
-        widen(0, pieces(10))
+        VW = [10, 16, 0, 0]
+        VB = {0: {(0, 1): (0,)}}
+        widen(0, pieces(VW[0]))
         for item in turns[:2]:
             quantize_x(*item, turn(*item, vector_banks=(1,)))
-        widen(1, pieces(5)[0::3])
+        widen(1, pieces(VW[1])[0::3])
         turned = []
         for k, (u, part) in enumerate(chunks):
             for item in turned:
@@ -247,10 +251,10 @@ def tile_crosslayerguidedstylegramlogcoshgrad_d1p_kernel(
                 finish(*pair)
             for pair in grams.get(k, ()):
                 gram(*pair)
-            turned = [item + (turn(*item, vector_banks=()),) for item in (turns[2:4] if k == 0 else turns[k + 3 : k + 4])]
+            turned = [item + (turn(*item, vector_banks=VB.get(k, {}).get(item, ())),) for item in (turns[2:4] if k == 0 else turns[k + 3 : k + 4])]
             nxt = (k + 1) // 3 + 1
             if nxt < UNITS:
-                widen(nxt, pieces(5)[(k + 1) % 3 :: 3])
+                widen(nxt, pieces(VW[nxt])[(k + 1) % 3 :: 3])
             leaky(u, part)
             if part == "f2":
                 sign(u)

@@ -24,6 +24,7 @@ NB = 512
 UNITS = B * S // KP
 G = S // KP
 SLOPE = 0.2
+YW = 512
 
 
 def tile_crosslayerguidedstylegramlogcoshgrad_d1p_kernel(
@@ -115,35 +116,43 @@ def tile_crosslayerguidedstylegramlogcoshgrad_d1p_kernel(
             nc.vector.quantize_mx(out=c[:].bitcast(FP8X4), scales=s[:], in_=grouped[:].rearrange("p c j -> p (c j)"))
             codes[u, kind], planes[u, kind] = c, s
 
-        def project(u, part):
-            yt = work.tile([P, T, NB], F32, name="y")
+        def project_f1(u, half):
+            yt = work.tile([P, T, YW], F32, name="y1")
+            words = w1c[:, 2 * NB * half : 2 * NB * (half + 1)].bitcast(FP4X4)
+            plane = w1p[:, NB * half : NB * (half + 1)]
             for t in range(T):
                 cols = slice(P * t, P * (t + 1))
                 bank = z_psum.tile([P, NB], F32, name="z_bank")
-                kinds = (0, 1) if part == "f2" else ("x1",)
-                for i, kind in enumerate(kinds):
-                    if part == "f2":
-                        words, plane = w2c[:, kind, :], w2p[:, kind, :]
-                    else:
-                        words = w1c[:, 2 * NB * part : 2 * NB * (part + 1)]
-                        plane = w1p[:, NB * part : NB * (part + 1)]
-                    nc.tensor.matmul_mx(
-                        out=bank[:],
-                        lhsT=codes[u, kind][:, cols].bitcast(FP8X4),
-                        lhsT_scale=planes[u, kind][:, cols],
-                        rhs=words.bitcast(FP4X4),
-                        rhs_scale=plane,
-                        start=(i == 0),
-                        stop=(i == len(kinds) - 1),
-                    )
-                if part == "f2":
-                    nc.scalar.copy(out=yt[:, t, :], in_=bank[:])
-                else:
-                    nc.scalar.activation(out=yt[:, t, :], in_=bank[:], func=ACT.Copy, scale=absm[:, u, t : t + 1])
-            y[u, part] = yt
+                nc.tensor.matmul_mx(
+                    out=bank[:], lhsT=codes[u, "x1"][:, cols].bitcast(FP8X4), lhsT_scale=planes[u, "x1"][:, cols],
+                    rhs=words, rhs_scale=plane, start=True, stop=True,
+                )
+                nc.scalar.activation(out=yt[:, t, 0:NB], in_=bank[:], func=ACT.Copy, scale=absm[:, u, t : t + 1])
+            y[u, half] = yt[:, :, 0:NB].rearrange("p t n -> p n t")
+
+        def project_f2(u):
+            yt = work.tile([P, NB, T], F32, name="y2")
+            for j in range(C2 // P):
+                bank = z_psum.tile([P, T, P], F32, name="z_bank")
+                for t in range(T):
+                    cols = slice(P * t, P * (t + 1))
+                    for kind in range(2):
+                        nc.tensor.matmul_mx(
+                            out=bank[:, t, :], lhsT=codes[u, kind][:, cols].bitcast(FP8X4), lhsT_scale=planes[u, kind][:, cols],
+                            rhs=w2c[:, kind, 2 * P * j : 2 * P * (j + 1)].bitcast(FP4X4),
+                            rhs_scale=w2p[:, kind, P * j : P * (j + 1)], start=(kind == 0), stop=(kind == 1),
+                        )
+                nc.scalar.copy(out=yt[:, P * j : P * (j + 1), :], in_=bank[:].rearrange("p t n -> p n t"))
+            y[u, "f2"] = yt[:]
+
+        def project(u, part):
+            if part == "f2":
+                project_f2(u)
+            else:
+                project_f1(u, part)
 
         def leaky(u, part):
-            src = y[u, part][:].rearrange("p t n -> p n t")
+            src = y[u, part]
             ft = work.tile([P, NB, T], BF16, name="f", align_bytes=64)
             nc.vector.scalar_tensor_tensor(out=ft[:], in0=src, scalar=SLOPE, in1=src, op0=ALU.mult, op1=ALU.max)
             f[u, part] = ft
@@ -234,8 +243,8 @@ def tile_crosslayerguidedstylegramlogcoshgrad_d1p_kernel(
             turns += [(u, 0), (u, 1), (u, "x1")]
         grams = {6: [(0, 0)], 7: [(0, 1)], 8: [(0, 2)], 9: [(0, 3)], 11: [(1, 0)]}
 
-        VW = [10, 16, 0, 0]
-        VB = {0: {(0, 1): (0,)}}
+        VW = [10, 8, 0, 0]
+        VB = {0: {(0, 1): (0, 1)}}
         widen(0, pieces(VW[0]))
         for item in turns[:2]:
             quantize_x(*item, turn(*item, vector_banks=(1,)))

@@ -24,7 +24,7 @@ NB = 512
 UNITS = B * S // KP
 G = S // KP
 SLOPE = 0.2
-YW = 512
+YW = 528
 
 
 def tile_crosslayerguidedstylegramlogcoshgrad_d1p_kernel(
@@ -68,11 +68,10 @@ def tile_crosslayerguidedstylegramlogcoshgrad_d1p_kernel(
             x1_in[u] = load.tile([P, T, D1], U8, name="x1_in")
             nc.sync.dma_start(out=x1_in[u][:], in_=unit_rows(x1_bytes, u))
 
-        def load_x2(u, halves=(0, 1)):
-            if u not in x2_in:
-                x2_in[u] = load.tile([P, T, D2], BF16, name="x2_in")
-            for h in halves:
-                k = slice(h * KP, (h + 1) * KP)
+        def load_x2(u, parts=1):
+            x2_in[u] = load.tile([P, T, D2], BF16, name="x2_in")
+            for h in range(parts):
+                k = slice(h * D2 // parts, (h + 1) * D2 // parts)
                 nc.sync.dma_start(out=x2_in[u][:, :, k], in_=unit_rows(x2, u)[:, :, k])
 
         def widen(u, pieces):
@@ -209,64 +208,73 @@ def tile_crosslayerguidedstylegramlogcoshgrad_d1p_kernel(
         load_x1(0)
         nc.sync.dma_start(out=x1s[:].rearrange("p u t j -> p u (t j)"),
                           in_=x1_scale.rearrange("b (g p t) j -> p (b g) (t j)", g=G, t=T))
-        load_x2(0, (0,))
+        load_x2(0, 2)
         nc.sync.dma_start(out=m_sb[:], in_=m.rearrange("b (g p t) -> p (b g) t", g=G, t=T))
         for q in range(4):
             nc.sync.dma_start(out=w1p[32 * q : 32 * q + 4, :].bitcast(I32),
                               in_=w1_scales[0, 4 * q : 4 * q + 4, :].bitcast(I32))
         nc.sync.dma_start(out=w1c[:].bitcast(I32), in_=w1_words[0].bitcast(I32))
-        load_x2(0, (1,))
         load_x1(1)
         for q in range(4):
             nc.sync.dma_start(out=w2p[32 * q : 32 * q + 4, :, :].bitcast(I32),
                               in_=w2_scales[:, 4 * q : 4 * q + 4, :].rearrange("g r n -> r g n").bitcast(I32))
         nc.sync.dma_start(out=w2c[:].bitcast(I32), in_=w2_words.rearrange("g p n -> p g n").bitcast(I32))
+        load_x2(1)
+        for u in range(2, UNITS):
+            load_x1(u)
+            load_x2(u)
+        for b in range(B):
+            nc.sync.dma_start(out=a_sb[:, b], in_=a[b].rearrange("(i p) n -> p i n", p=P))
         nc.scalar.activation(out=warm[:], in_=zero[:], func=ACT.Tanh)
         nc.gpsimd.tensor_scalar(out=sgn2[:], in0=m_sb[:], scalar1=0.0, scalar2=2.0, op0=ALU.is_ge, op1=ALU.mult)
         nc.gpsimd.tensor_scalar(out=sgn[:], in0=sgn2[:], scalar1=1.0, scalar2=0.0, op0=ALU.subtract, op1=ALU.add)
         nc.gpsimd.tensor_tensor(out=absm[:], in0=m_sb[:], in1=sgn[:], op=ALU.mult)
-        for u in range(1, UNITS):
-            if u > 1:
-                load_x1(u)
-            load_x2(u)
-        for b in range(B):
-            nc.sync.dma_start(out=a_sb[:, b], in_=a[b].rearrange("(i p) n -> p i n", p=P))
 
         def pieces(v_count):
             order = [(t, j) for t in range(T) for j in range(4)]
             return [(t, j, (n * v_count) // 16 != ((n + 1) * v_count) // 16) for n, (t, j) in enumerate(order)]
 
-        chunks = [(0, 0), (0, 1), (0, "f2")]
-        turns = [(0, "x1"), (0, 0), (0, 1)]
-        for u in range(1, UNITS):
-            chunks += [(u, "f2"), (u, 0), (u, 1)]
-            turns += [(u, 0), (u, 1), (u, "x1")]
-        grams = {6: [(0, 0)], 7: [(0, 1)], 8: [(0, 2)], 9: [(0, 3)], 11: [(1, 0)]}
+        chunks, turns = [], []
+        for u in range(UNITS):
+            if u < UNITS - 1:
+                chunks += [(u, 0), (u, 1), (u, "f2")]
+                turns += [(u, "x1"), (u, 0), (u, 1)]
+            else:
+                chunks += [(u, "f2"), (u, 0), (u, 1)]
+                turns += [(u, 0), (u, 1), (u, "x1")]
+        turns_at = {0: [2], 1: [3], 2: [4], 3: [5], 4: [6], 5: [7, 8], 6: [9], 7: [10], 8: [11]}
+        grams = {7: [(0, 0)], 8: [(0, 1)], 9: [(0, 2)], 10: [(0, 3)], 11: [(1, 0)]}
+        widen_at = {-1: (1, 0, 2, 16), 0: (1, 1, 2, 8), 1: (2, 0, 3, 0), 2: (2, 1, 3, 0), 3: (2, 2, 3, 0), 5: (3, 0, 3, 0), 6: (3, 1, 3, 0), 7: (3, 2, 3, 0)}
+        VW = [10]
+        VB = {}
 
-        VW = [10, 8, 0, 0]
-        VB = {0: {(0, 1): (0, 1)}}
+        def widen_step(k):
+            if k in widen_at:
+                u, i, n, v = widen_at[k]
+                widen(u, pieces(v)[i::n])
+
         widen(0, pieces(VW[0]))
         for item in turns[:2]:
             quantize_x(*item, turn(*item, vector_banks=(1,)))
-        widen(1, pieces(VW[1])[0::3])
+        widen_step(-1)
         turned = []
         for k, (u, part) in enumerate(chunks):
             for item in turned:
                 quantize_x(*item)
-            if k > 0:
+            if k > 0 and chunks[k - 1][1] == "f2":
+                sign(chunks[k - 1][0])
+            elif k > 0:
                 quantize_f(*chunks[k - 1])
             project(u, part)
             for pair in grams.get(k - 1, ()):
                 finish(*pair)
             for pair in grams.get(k, ()):
                 gram(*pair)
-            turned = [item + (turn(*item, vector_banks=VB.get(k, {}).get(item, ())),) for item in (turns[2:4] if k == 0 else turns[k + 3 : k + 4])]
-            nxt = (k + 1) // 3 + 1
-            if nxt < UNITS:
-                widen(nxt, pieces(VW[nxt])[(k + 1) % 3 :: 3])
+            turned = [turns[j] + (turn(*turns[j], vector_banks=VB.get(k, {}).get(turns[j], ())),) for j in turns_at.get(k, ())]
+            widen_step(k)
             leaky(u, part)
-            if part == "f2":
-                sign(u)
+            if k > 0 and chunks[k - 1][1] == "f2":
+                quantize_f(*chunks[k - 1])
         quantize_f(*chunks[-1])
         for pair in grams[11]:
             finish(*pair)

@@ -19,12 +19,16 @@ FLOPS = 2 * B * S * (D1 * C1 + D2 * C2 + C1 * C2)
 
 P = 128
 T = 4
-KP = P * T
-NB = 512
-UNITS = B * S // KP
-G = S // KP
+PASS = P * T
+GROUPS_B = S // PASS
+GROUPS = B * GROUPS_B
+BANK = 512
+CHAN = 4
+K_SCALE = 128
 SLOPE = 0.2
-YW = 528
+
+PIECES = T * (D1 // K_SCALE)
+VECTOR_PIECES = 10
 
 
 def tile_crosslayerguidedstylegramlogcoshgrad_d1p_kernel(
@@ -33,251 +37,268 @@ def tile_crosslayerguidedstylegramlogcoshgrad_d1p_kernel(
     nc = tc.nc
     with ExitStack() as ctx:
         keep = ctx.enter_context(tc.tile_pool(name="keep", bufs=1))
-        load = ctx.enter_context(tc.tile_pool(name="load", bufs=UNITS))
+        load = ctx.enter_context(tc.tile_pool(name="load", bufs=GROUPS))
         work = ctx.enter_context(tc.tile_pool(name="work", bufs=3))
         code = ctx.enter_context(tc.tile_pool(name="code", bufs=2))
-        tr_psum = ctx.enter_context(tc.psum_pool(name="tr_psum", bufs=2))
+        x_psum = ctx.enter_context(tc.psum_pool(name="x_psum", bufs=2))
         z_psum = ctx.enter_context(tc.psum_pool(name="z_psum", bufs=4))
-        g_psum = ctx.enter_context(tc.psum_pool(name="g_psum", bufs=2))
+        gram_psum = ctx.enter_context(tc.psum_pool(name="gram_psum", bufs=2))
 
         ident = keep.tile([P, P], F32)
-        warm = keep.tile([P, 1], F32)
         zero = keep.tile([P, 1], F32)
-        x1s = keep.tile([P, UNITS, T, 4], F32)
-        m_sb = keep.tile([P, UNITS, T], BF16)
-        sgn2 = keep.tile([P, UNITS, T], F32)
-        sgn = keep.tile([P, UNITS, T], BF16)
-        absm = keep.tile([P, UNITS, T], F32)
-        w1c = keep.tile([P, 2 * C1], U8, align_bytes=64)
-        w1p = keep.tile([P, C1], U8, align_bytes=64)
-        w2c = keep.tile([P, 2, 2 * C2], U8, align_bytes=64)
-        w2p = keep.tile([P, 2, C2], U8, align_bytes=64)
-        a_sb = keep.tile([P, B, C1 // P, C2], BF16)
-        f1c = keep.tile([P, B, G, C1], U32, align_bytes=64)
-        f1p = keep.tile([P, B, G, C1], U8, align_bytes=64)
-        f2c = keep.tile([P, B, G, C2], U32, align_bytes=64)
-        f2p = keep.tile([P, B, G, C2], U8, align_bytes=64)
+        tanh_zero = keep.tile([P, 1], F32)
+        x1_scale_sb = keep.tile([P, GROUPS, T, D1 // K_SCALE], F32)
+        m_sb = keep.tile([P, GROUPS, T], BF16)
+        twice_positive = keep.tile([P, GROUPS, T], F32)
+        sign_m = keep.tile([P, GROUPS, T], BF16)
+        abs_m = keep.tile([P, GROUPS, T], F32)
+        w1_sb = keep.tile([P, 2 * C1], U8, align_bytes=64)
+        w1_scale_sb = keep.tile([P, C1], U8, align_bytes=64)
+        w2_sb = keep.tile([P, D2 // PASS, 2 * C2], U8, align_bytes=64)
+        w2_scale_sb = keep.tile([P, D2 // PASS, C2], U8, align_bytes=64)
+        a_sb = keep.tile([P, B, C1 // BANK, CHAN, C2], BF16)
+        fm_codes = keep.tile([P, B, GROUPS_B, C1], U32, align_bytes=64)
+        fm_scales = keep.tile([P, B, GROUPS_B, C1], U8, align_bytes=64)
+        f2_codes = keep.tile([P, B, GROUPS_B, C2], U32, align_bytes=64)
+        f2_scales = keep.tile([P, B, GROUPS_B, C2], U8, align_bytes=64)
 
         x1_in, x1_bf, x2_in = {}, {}, {}
-        codes, planes, y, f, o_tiles = {}, {}, {}, {}, {}
+        x_codes, x_scales, y, f, result = {}, {}, {}, {}, {}
 
-        def unit_rows(src, u):
-            return src[u // G, (u % G) * KP : (u % G + 1) * KP].rearrange("(p t) k -> p t k", t=T)
+        def group_rows(src, u):
+            g = u % GROUPS_B
+            return src[u // GROUPS_B, g * PASS : (g + 1) * PASS].rearrange("(p t) k -> p t k", t=T)
 
         def load_x1(u):
             x1_in[u] = load.tile([P, T, D1], U8, name="x1_in")
-            nc.sync.dma_start(out=x1_in[u][:], in_=unit_rows(x1_bytes, u))
+            nc.sync.dma_start(out=x1_in[u][:], in_=group_rows(x1_bytes, u))
 
-        def load_x2(u, parts=1):
+        def load_x2(u, parts):
             x2_in[u] = load.tile([P, T, D2], BF16, name="x2_in")
             for h in range(parts):
                 k = slice(h * D2 // parts, (h + 1) * D2 // parts)
-                nc.sync.dma_start(out=x2_in[u][:, :, k], in_=unit_rows(x2, u)[:, :, k])
+                nc.sync.dma_start(out=x2_in[u][:, :, k], in_=group_rows(x2, u)[:, :, k])
 
-        def widen(u, pieces):
+        def load_scales(tile_rows, rows):
+            for q in range(4):
+                nc.sync.dma_start(out=tile_rows(slice(32 * q, 32 * q + 4)).bitcast(I32), in_=rows(slice(4 * q, 4 * q + 4)))
+
+        def widen(u, pieces, on_vector):
             if u not in x1_bf:
                 x1_bf[u] = work.tile([P, T, D1], BF16, name="x1_bf")
-            for t, j, on_vector in pieces:
-                cols = slice(P * j, P * (j + 1))
+            for piece in pieces:
+                t, j = divmod(piece, D1 // K_SCALE)
+                cols = slice(K_SCALE * j, K_SCALE * (j + 1))
+                dst = x1_bf[u][:, t, cols]
                 src = x1_in[u][:, t, cols].bitcast(FP8)
-                scale = x1s[:, u, t, j : j + 1]
-                if on_vector:
-                    nc.vector.tensor_scalar(out=x1_bf[u][:, t, cols], in0=src, scalar1=scale, scalar2=None, op0=ALU.mult)
+                scale = x1_scale_sb[:, u, t, j : j + 1]
+                if on_vector(piece):
+                    nc.vector.tensor_scalar(out=dst, in0=src, scalar1=scale, scalar2=None, op0=ALU.mult)
                 else:
-                    nc.scalar.activation(out=x1_bf[u][:, t, cols], in_=src, func=ACT.Copy, scale=scale)
+                    nc.scalar.activation(out=dst, in_=src, func=ACT.Copy, scale=scale)
 
-        def turn(u, kind, vector_banks=()):
-            if kind == "x1":
-                words = x1_bf[u][:].rearrange("p t k -> p (t k)").bitcast(F32)
-                row, first = D1 // 2, 0
-            else:
-                words = x2_in[u][:].rearrange("p t k -> p (t k)").bitcast(F32)
-                row, first = D2 // 2, (KP // 2) * kind
-            grouped = work.tile([P, KP, T], BF16, name="x_grouped", align_bytes=64)
-            gw = grouped[:].rearrange("p c j -> p (c j)").bitcast(F32)
-            for pair in range(2):
-                bank = tr_psum.tile([P, 2, 2, P], F32, name="x_bank")
+        def turn(u, operand, last_bank_on_vector=False):
+            src, g = (x1_bf[u], 0) if operand == "x1" else (x2_in[u], operand)
+            row = src.shape[2] // 2
+            words = src[:].rearrange("p t k -> p (t k)").bitcast(F32)
+            turned = work.tile([P, PASS, T], BF16, name="x_turned", align_bytes=64)
+            turned_words = turned[:].rearrange("p c j -> p (c j)").bitcast(F32)
+            for half in range(2):
+                bank = x_psum.tile([P, 2, 2, P], F32, name="x_bank")
                 for i in range(2):
                     for e in range(2):
-                        at = row * (2 * pair + i) + first + e
-                        nc.tensor.transpose(bank[:, i, e, :], words[:, at : at + KP // 2 - 1 : 2], ident[:])
-                dst = gw[:, KP * pair : KP * (pair + 1)].rearrange("p (i r e) -> p i r e", i=2, e=2)
-                src = bank[:].rearrange("p i e r -> p i r e")
-                if pair in vector_banks:
-                    nc.vector.tensor_copy(out=dst, in_=src)
+                        at = row * (2 * half + i) + PASS // 2 * g + e
+                        nc.tensor.transpose(bank[:, i, e, :], words[:, at : at + PASS // 2 - 1 : 2], ident[:])
+                dst = turned_words[:, PASS * half : PASS * (half + 1)].rearrange("p (i r e) -> p i r e", i=2, e=2)
+                if half == 1 and last_bank_on_vector:
+                    nc.vector.tensor_copy(out=dst, in_=bank[:].rearrange("p i e r -> p i r e"))
                 else:
-                    nc.scalar.copy(out=dst, in_=src)
-            return grouped
+                    nc.scalar.copy(out=dst, in_=bank[:].rearrange("p i e r -> p i r e"))
+            return turned
 
-        def quantize_x(u, kind, grouped):
-            c = code.tile([P, KP], U32, name="c_%s" % kind, align_bytes=64)
-            s = code.tile([P, KP], U8, name="s_%s" % kind, align_bytes=64)
-            nc.vector.quantize_mx(out=c[:].bitcast(FP8X4), scales=s[:], in_=grouped[:].rearrange("p c j -> p (c j)"))
-            codes[u, kind], planes[u, kind] = c, s
+        def quantize_x(u, operand, turned):
+            codes = code.tile([P, PASS], U32, name="codes_%s" % operand, align_bytes=64)
+            scales = code.tile([P, PASS], U8, name="scales_%s" % operand, align_bytes=64)
+            nc.vector.quantize_mx(
+                out=codes[:].bitcast(FP8X4), scales=scales[:], in_=turned[:].rearrange("p c j -> p (c j)")
+            )
+            x_codes[u, operand], x_scales[u, operand] = codes, scales
 
-        def project_f1(u, half):
-            yt = work.tile([P, T, YW], F32, name="y1")
-            words = w1c[:, 2 * NB * half : 2 * NB * (half + 1)].bitcast(FP4X4)
-            plane = w1p[:, NB * half : NB * (half + 1)]
+        def multiply(bank, u, operand, t, words, word_scales, start, stop):
+            cols = slice(P * t, P * (t + 1))
+            nc.tensor.matmul_mx(
+                out=bank,
+                lhsT=x_codes[u, operand][:, cols].bitcast(FP8X4),
+                lhsT_scale=x_scales[u, operand][:, cols],
+                rhs=words.bitcast(FP4X4),
+                rhs_scale=word_scales,
+                start=start,
+                stop=stop,
+            )
+
+        def project_fm(u, h):
+            y[u, h] = work.tile([P, P, T, CHAN], F32, name="y1")
+            cols = slice(BANK * h, BANK * (h + 1))
             for t in range(T):
-                cols = slice(P * t, P * (t + 1))
-                bank = z_psum.tile([P, NB], F32, name="z_bank")
-                nc.tensor.matmul_mx(
-                    out=bank[:], lhsT=codes[u, "x1"][:, cols].bitcast(FP8X4), lhsT_scale=planes[u, "x1"][:, cols],
-                    rhs=words, rhs_scale=plane, start=True, stop=True,
+                bank = z_psum.tile([P, BANK], F32, name="z_bank")
+                multiply(
+                    bank[:], u, "x1", t, w1_sb[:, 2 * BANK * h : 2 * BANK * (h + 1)], w1_scale_sb[:, cols], True, True
                 )
-                nc.scalar.activation(out=yt[:, t, 0:NB], in_=bank[:], func=ACT.Copy, scale=absm[:, u, t : t + 1])
-            y[u, half] = yt[:, :, 0:NB].rearrange("p t n -> p n t")
+                nc.scalar.activation(
+                    out=y[u, h][:, :, t, :],
+                    in_=bank[:].rearrange("p (c i) -> p c i", i=CHAN),
+                    func=ACT.Copy,
+                    scale=abs_m[:, u, t : t + 1],
+                )
 
         def project_f2(u):
-            yt = work.tile([P, NB, T], F32, name="y2")
+            y[u, "f2"] = work.tile([P, C2, T], F32, name="y2")
             for j in range(C2 // P):
+                cols = slice(P * j, P * (j + 1))
                 bank = z_psum.tile([P, T, P], F32, name="z_bank")
                 for t in range(T):
-                    cols = slice(P * t, P * (t + 1))
-                    for kind in range(2):
-                        nc.tensor.matmul_mx(
-                            out=bank[:, t, :], lhsT=codes[u, kind][:, cols].bitcast(FP8X4), lhsT_scale=planes[u, kind][:, cols],
-                            rhs=w2c[:, kind, 2 * P * j : 2 * P * (j + 1)].bitcast(FP4X4),
-                            rhs_scale=w2p[:, kind, P * j : P * (j + 1)], start=(kind == 0), stop=(kind == 1),
-                        )
-                nc.scalar.copy(out=yt[:, P * j : P * (j + 1), :], in_=bank[:].rearrange("p t n -> p n t"))
-            y[u, "f2"] = yt[:]
+                    for g in range(2):
+                        words = w2_sb[:, g, 2 * P * j : 2 * P * (j + 1)]
+                        multiply(bank[:, t, :], u, g, t, words, w2_scale_sb[:, g, cols], g == 0, g == 1)
+                nc.scalar.copy(out=y[u, "f2"][:, cols, :], in_=bank[:].rearrange("p t n -> p n t"))
 
-        def project(u, part):
+        def leaky(u, part):
+            f[u, part] = work.tile([P, BANK, T], BF16, name="f", align_bytes=64)
+            if part == "f2":
+                src, dst = y[u, part][:], f[u, part][:]
+            else:
+                src = y[u, part][:].rearrange("p c t i -> p (c t) i")
+                dst = f[u, part][:].rearrange("p (i c) t -> p (c t) i", i=CHAN)
+            nc.vector.scalar_tensor_tensor(out=dst, in0=src, scalar=SLOPE, in1=src, op0=ALU.mult, op1=ALU.max)
+
+        def apply_sign(u):
+            signed = work.tile([P, C2, T], BF16, name="f2_signed", align_bytes=64)
+            signs = sign_m[:, u, :].unsqueeze(1).to_broadcast([P, C2, T])
+            nc.vector.tensor_tensor(out=signed[:], in0=f[u, "f2"][:], in1=signs, op=ALU.mult)
+            f[u, "f2"] = signed
+
+        def quantize_f(u, part):
+            b, g = divmod(u, GROUPS_B)
+            if part == "f2":
+                codes, scales = f2_codes[:, b, g, :], f2_scales[:, b, g, :]
+            else:
+                cols = slice(BANK * part, BANK * (part + 1))
+                codes, scales = fm_codes[:, b, g, cols], fm_scales[:, b, g, cols]
+            nc.vector.quantize_mx(
+                out=codes.bitcast(FP8X4), scales=scales, in_=f[u, part][:].rearrange("p n t -> p (n t)")
+            )
+
+        def gram_pair(b, pair):
+            h, i0 = divmod(2 * pair, CHAN)
+            result[b, pair] = work.tile([P, 2, C2], F32, name="result")
+            for i in range(2):
+                bank = gram_psum.tile([P, C2], F32, name="gram_bank")
+                cols = slice(P * (2 * pair + i), P * (2 * pair + i + 1))
+                for g in range(GROUPS_B):
+                    nc.tensor.matmul_mx(
+                        out=bank[:],
+                        lhsT=fm_codes[:, b, g, cols].bitcast(FP8X4),
+                        lhsT_scale=fm_scales[:, b, g, cols],
+                        rhs=f2_codes[:, b, g, :].bitcast(FP8X4),
+                        rhs_scale=f2_scales[:, b, g, :],
+                        start=(g == 0),
+                        stop=(g == GROUPS_B - 1),
+                    )
+                nc.vector.scalar_tensor_tensor(
+                    out=result[b, pair][:, i, :],
+                    in0=bank[:],
+                    scalar=1.0 / 32.0,
+                    in1=a_sb[:, b, h, i0 + i, :],
+                    op0=ALU.mult,
+                    op1=ALU.subtract,
+                )
+
+        def finish_pair(b, pair, blocks):
+            h, i0 = divmod(2 * pair, CHAN)
+            rows = out[b, BANK * h : BANK * (h + 1)].rearrange("(c i) n -> c i n", i=CHAN)
+            for i in range(0, 2, blocks):
+                block = result[b, pair][:, i : i + blocks]
+                nc.scalar.activation(out=block, in_=block, func=ACT.Tanh)
+                nc.sync.dma_start(out=rows[:, i0 + i : i0 + i + blocks], in_=block)
+
+        ctx.enter_context(tc.manual_schedule())
+
+        nc.vector.memset(zero[:], 0.0)
+        nc.vector.memset(w1_scale_sb[:].bitcast(I32), 0)
+        nc.vector.memset(w2_scale_sb[:].rearrange("p g n -> p (g n)").bitcast(I32), 0)
+        make_identity(nc, ident[:])
+        load_x1(0)
+        nc.sync.dma_start(
+            out=x1_scale_sb[:].rearrange("p u t j -> p u (t j)"),
+            in_=x1_scale.rearrange("b (g p t) j -> p (b g) (t j)", g=GROUPS_B, t=T),
+        )
+        load_x2(0, 2)
+        nc.sync.dma_start(out=m_sb[:], in_=m.rearrange("b (g p t) -> p (b g) t", g=GROUPS_B, t=T))
+        load_scales(lambda p: w1_scale_sb[p, :], lambda r: w1_scales[0, r, :].bitcast(I32))
+        nc.sync.dma_start(out=w1_sb[:].bitcast(I32), in_=w1_words[0].bitcast(I32))
+        load_x1(1)
+        load_scales(lambda p: w2_scale_sb[p, :, :], lambda r: w2_scales[:, r, :].rearrange("g r n -> r g n").bitcast(I32))
+        nc.sync.dma_start(out=w2_sb[:].bitcast(I32), in_=w2_words.rearrange("g p n -> p g n").bitcast(I32))
+        load_x2(1, 1)
+        for u in range(2, GROUPS):
+            load_x1(u)
+            load_x2(u, 1)
+        for b in range(B):
+            nc.sync.dma_start(out=a_sb[:, b], in_=a[b].rearrange("(h c i) n -> c h i n", c=P, i=CHAN))
+        nc.scalar.activation(out=tanh_zero[:], in_=zero[:], func=ACT.Tanh)
+        nc.gpsimd.tensor_scalar(out=twice_positive[:], in0=m_sb[:], scalar1=tanh_zero[:], scalar2=2.0, op0=ALU.is_ge, op1=ALU.mult)
+        nc.gpsimd.tensor_scalar(out=sign_m[:], in0=twice_positive[:], scalar1=1.0, scalar2=0.0, op0=ALU.subtract, op1=ALU.add)
+        nc.gpsimd.tensor_tensor(out=abs_m[:], in0=m_sb[:], in1=sign_m[:], op=ALU.mult)
+
+        steps, to_turn = [], []
+        for u in range(GROUPS):
+            f2_first = u == GROUPS - 1
+            steps += [(u, "f2"), (u, 0), (u, 1)] if f2_first else [(u, 0), (u, 1), (u, "f2")]
+            to_turn += [(u, 0), (u, 1), (u, "x1")] if f2_first else [(u, "x1"), (u, 0), (u, 1)]
+        two_turns_step = 5
+        widen_in_step = {0: (1, range(1, PIECES, 2))}
+        for third in range(3):
+            widen_in_step[1 + third] = (2, range(third, PIECES, 3))
+            widen_in_step[5 + third] = (3, range(third, PIECES, 3))
+        pairs = C1 // P // 2
+        pair_in_step = {7 + pair: (0, pair) for pair in range(pairs)}
+        pair_in_step[len(steps) - 1] = (1, 0)
+
+        widen(0, range(PIECES), lambda n: n * VECTOR_PIECES // PIECES != (n + 1) * VECTOR_PIECES // PIECES)
+        for operand in to_turn[:2]:
+            quantize_x(*operand, turn(*operand, last_bank_on_vector=True))
+        widen(1, range(0, PIECES, 2), lambda n: True)
+        n_turned = 2
+
+        turned = []
+        for k, (u, part) in enumerate(steps):
+            for operand, tile in turned:
+                quantize_x(*operand, tile)
+            signed = steps[k - 1] if k > 0 and steps[k - 1][1] == "f2" else None
+            if signed:
+                apply_sign(signed[0])
+            elif k > 0:
+                quantize_f(*steps[k - 1])
+
             if part == "f2":
                 project_f2(u)
             else:
-                project_f1(u, part)
+                project_fm(u, part)
+            if k - 1 in pair_in_step:
+                finish_pair(*pair_in_step[k - 1], 2)
+            if k in pair_in_step:
+                gram_pair(*pair_in_step[k])
 
-        def leaky(u, part):
-            src = y[u, part]
-            ft = work.tile([P, NB, T], BF16, name="f", align_bytes=64)
-            nc.vector.scalar_tensor_tensor(out=ft[:], in0=src, scalar=SLOPE, in1=src, op0=ALU.mult, op1=ALU.max)
-            f[u, part] = ft
-
-        def sign(u):
-            ft = work.tile([P, NB, T], BF16, name="f_signed", align_bytes=64)
-            nc.vector.tensor_tensor(
-                out=ft[:], in0=f[u, "f2"][:], in1=sgn[:, u, :].unsqueeze(1).to_broadcast([P, NB, T]), op=ALU.mult
-            )
-            f[u, "f2"] = ft
-
-        def quantize_f(u, part):
-            b, g = u // G, u % G
-            if part == "f2":
-                c, s = f2c[:, b, g, :], f2p[:, b, g, :]
-            else:
-                cols = slice(NB * part, NB * (part + 1))
-                c, s = f1c[:, b, g, cols], f1p[:, b, g, cols]
-            nc.vector.quantize_mx(out=c.bitcast(FP8X4), scales=s, in_=f[u, part][:].rearrange("p n t -> p (n t)"))
-
-        def gram(b, pair):
-            o = work.tile([P, 2, C2], F32, name="o")
-            o_tiles[b, pair] = o
-            for i in range(2):
-                ib = 2 * pair + i
-                bank = g_psum.tile([P, C2], F32, name="g_bank")
-                for g in range(G):
-                    cols = slice(P * ib, P * (ib + 1))
-                    nc.tensor.matmul_mx(
-                        out=bank[:],
-                        lhsT=f1c[:, b, g, cols].bitcast(FP8X4),
-                        lhsT_scale=f1p[:, b, g, cols],
-                        rhs=f2c[:, b, g, :].bitcast(FP8X4),
-                        rhs_scale=f2p[:, b, g, :],
-                        start=(g == 0),
-                        stop=(g == G - 1),
-                    )
-                nc.vector.scalar_tensor_tensor(
-                    out=o[:, i, :], in0=bank[:], scalar=1.0 / 32.0, in1=a_sb[:, b, ib, :], op0=ALU.mult, op1=ALU.subtract
-                )
-
-        def finish(b, pair, step=2):
-            o = o_tiles[b, pair]
-            rows = out[b, 2 * P * pair : 2 * P * (pair + 1)].rearrange("(i p) n -> p i n", p=P)
-            for i in range(0, 2, step):
-                nc.scalar.activation(out=o[:, i : i + step], in_=o[:, i : i + step], func=ACT.Tanh)
-                nc.sync.dma_start(out=rows[:, i : i + step], in_=o[:, i : i + step])
-
-        ctx.enter_context(tc.manual_schedule())
-        nc.vector.memset(zero[:], 0.0)
-        nc.vector.memset(w1p[:].bitcast(I32), 0)
-        nc.vector.memset(w2p[:].rearrange("p g n -> p (g n)").bitcast(I32), 0)
-        make_identity(nc, ident[:])
-        load_x1(0)
-        nc.sync.dma_start(out=x1s[:].rearrange("p u t j -> p u (t j)"),
-                          in_=x1_scale.rearrange("b (g p t) j -> p (b g) (t j)", g=G, t=T))
-        load_x2(0, 2)
-        nc.sync.dma_start(out=m_sb[:], in_=m.rearrange("b (g p t) -> p (b g) t", g=G, t=T))
-        for q in range(4):
-            nc.sync.dma_start(out=w1p[32 * q : 32 * q + 4, :].bitcast(I32),
-                              in_=w1_scales[0, 4 * q : 4 * q + 4, :].bitcast(I32))
-        nc.sync.dma_start(out=w1c[:].bitcast(I32), in_=w1_words[0].bitcast(I32))
-        load_x1(1)
-        for q in range(4):
-            nc.sync.dma_start(out=w2p[32 * q : 32 * q + 4, :, :].bitcast(I32),
-                              in_=w2_scales[:, 4 * q : 4 * q + 4, :].rearrange("g r n -> r g n").bitcast(I32))
-        nc.sync.dma_start(out=w2c[:].bitcast(I32), in_=w2_words.rearrange("g p n -> p g n").bitcast(I32))
-        load_x2(1)
-        for u in range(2, UNITS):
-            load_x1(u)
-            load_x2(u)
-        for b in range(B):
-            nc.sync.dma_start(out=a_sb[:, b], in_=a[b].rearrange("(i p) n -> p i n", p=P))
-        nc.scalar.activation(out=warm[:], in_=zero[:], func=ACT.Tanh)
-        nc.gpsimd.tensor_scalar(out=sgn2[:], in0=m_sb[:], scalar1=0.0, scalar2=2.0, op0=ALU.is_ge, op1=ALU.mult)
-        nc.gpsimd.tensor_scalar(out=sgn[:], in0=sgn2[:], scalar1=1.0, scalar2=0.0, op0=ALU.subtract, op1=ALU.add)
-        nc.gpsimd.tensor_tensor(out=absm[:], in0=m_sb[:], in1=sgn[:], op=ALU.mult)
-
-        def pieces(v_count):
-            order = [(t, j) for t in range(T) for j in range(4)]
-            return [(t, j, (n * v_count) // 16 != ((n + 1) * v_count) // 16) for n, (t, j) in enumerate(order)]
-
-        chunks, turns = [], []
-        for u in range(UNITS):
-            if u < UNITS - 1:
-                chunks += [(u, 0), (u, 1), (u, "f2")]
-                turns += [(u, "x1"), (u, 0), (u, 1)]
-            else:
-                chunks += [(u, "f2"), (u, 0), (u, 1)]
-                turns += [(u, 0), (u, 1), (u, "x1")]
-        turns_at = {0: [2], 1: [3], 2: [4], 3: [5], 4: [6], 5: [7, 8], 6: [9], 7: [10], 8: [11]}
-        grams = {7: [(0, 0)], 8: [(0, 1)], 9: [(0, 2)], 10: [(0, 3)], 11: [(1, 0)]}
-        widen_at = {-1: (1, 0, 2, 16), 0: (1, 1, 2, 8), 1: (2, 0, 3, 0), 2: (2, 1, 3, 0), 3: (2, 2, 3, 0), 5: (3, 0, 3, 0), 6: (3, 1, 3, 0), 7: (3, 2, 3, 0)}
-        VW = [10]
-        VB = {}
-
-        def widen_step(k):
-            if k in widen_at:
-                u, i, n, v = widen_at[k]
-                widen(u, pieces(v)[i::n])
-
-        widen(0, pieces(VW[0]))
-        for item in turns[:2]:
-            quantize_x(*item, turn(*item, vector_banks=(1,)))
-        widen_step(-1)
-        turned = []
-        for k, (u, part) in enumerate(chunks):
-            for item in turned:
-                quantize_x(*item)
-            if k > 0 and chunks[k - 1][1] == "f2":
-                sign(chunks[k - 1][0])
-            elif k > 0:
-                quantize_f(*chunks[k - 1])
-            project(u, part)
-            for pair in grams.get(k - 1, ()):
-                finish(*pair)
-            for pair in grams.get(k, ()):
-                gram(*pair)
-            turned = [turns[j] + (turn(*turns[j], vector_banks=VB.get(k, {}).get(turns[j], ())),) for j in turns_at.get(k, ())]
-            widen_step(k)
+            first, n_turned = n_turned, n_turned + (2 if k == two_turns_step else 1)
+            turned = [(operand, turn(*operand)) for operand in to_turn[first:n_turned]]
+            if k in widen_in_step:
+                widen(*widen_in_step[k], lambda n, group=widen_in_step[k][0]: group == 1)
             leaky(u, part)
-            if k > 0 and chunks[k - 1][1] == "f2":
-                quantize_f(*chunks[k - 1])
-        quantize_f(*chunks[-1])
-        for pair in grams[11]:
-            finish(*pair)
-        for pair in range(4 - len(grams[11])):
-            gram(1, len(grams[11]) + pair)
-            finish(1, len(grams[11]) + pair, 1)
+            if signed:
+                quantize_f(*signed)
+
+        quantize_f(*steps[-1])
+        finish_pair(1, 0, 2)
+        for pair in range(1, pairs):
+            gram_pair(1, pair)
+            finish_pair(1, pair, 1)

from contextlib import ExitStack

import concourse.mybir as mybir
from concourse.masks import make_identity

F32 = mybir.dt.float32
BF16 = mybir.dt.bfloat16
I32 = mybir.dt.int32
U32 = mybir.dt.uint32
U8 = mybir.dt.uint8
FP8 = mybir.dt.float8_e4m3fn
FP8X4 = mybir.dt.float8_e4m3fn_x4
FP4X4 = mybir.dt.float4_e2m1fn_x4
ALU = mybir.AluOpType
ACT = mybir.ActivationFunctionType

B, S, D1, D2, C1, C2 = 2, 1024, 512, 1024, 1024, 512
FLOPS = 2 * B * S * (D1 * C1 + D2 * C2 + C1 * C2)

P = 128
T = 4
PASS = P * T
GROUPS_B = S // PASS
GROUPS = B * GROUPS_B
BANK = 512
CHAN = 4
K_SCALE = 128
SLOPE = 0.2

PIECES = T * (D1 // K_SCALE)
VECTOR_PIECES = 10


def tile_crosslayerguidedstylegramlogcoshgrad_d1p_kernel(
    tc, x1_bytes, x1_scale, x2, w1_words, w1_scales, w2_words, w2_scales, m, a, out
):
    nc = tc.nc
    with ExitStack() as ctx:
        keep = ctx.enter_context(tc.tile_pool(name="keep", bufs=1))
        load = ctx.enter_context(tc.tile_pool(name="load", bufs=GROUPS))
        work = ctx.enter_context(tc.tile_pool(name="work", bufs=3))
        code = ctx.enter_context(tc.tile_pool(name="code", bufs=2))
        x_psum = ctx.enter_context(tc.psum_pool(name="x_psum", bufs=2))
        z_psum = ctx.enter_context(tc.psum_pool(name="z_psum", bufs=4))
        gram_psum = ctx.enter_context(tc.psum_pool(name="gram_psum", bufs=2))

        ident = keep.tile([P, P], F32)
        zero = keep.tile([P, 1], F32)
        tanh_zero = keep.tile([P, 1], F32)
        x1_scale_sb = keep.tile([P, GROUPS, T, D1 // K_SCALE], F32)
        m_sb = keep.tile([P, GROUPS, T], BF16)
        twice_positive = keep.tile([P, GROUPS, T], F32)
        sign_m = keep.tile([P, GROUPS, T], BF16)
        abs_m = keep.tile([P, GROUPS, T], F32)
        w1_sb = keep.tile([P, 2 * C1], U8, align_bytes=64)
        w1_scale_sb = keep.tile([P, C1], U8, align_bytes=64)
        w2_sb = keep.tile([P, D2 // PASS, 2 * C2], U8, align_bytes=64)
        w2_scale_sb = keep.tile([P, D2 // PASS, C2], U8, align_bytes=64)
        a_sb = keep.tile([P, B, C1 // BANK, CHAN, C2], BF16)
        fm_codes = keep.tile([P, B, GROUPS_B, C1], U32, align_bytes=64)
        fm_scales = keep.tile([P, B, GROUPS_B, C1], U8, align_bytes=64)
        f2_codes = keep.tile([P, B, GROUPS_B, C2], U32, align_bytes=64)
        f2_scales = keep.tile([P, B, GROUPS_B, C2], U8, align_bytes=64)

        x1_in, x1_bf, x2_in = {}, {}, {}
        x_codes, x_scales, y, f, result = {}, {}, {}, {}, {}

        def group_rows(src, u):
            g = u % GROUPS_B
            return src[u // GROUPS_B, g * PASS : (g + 1) * PASS].rearrange("(p t) k -> p t k", t=T)

        def load_x1(u):
            x1_in[u] = load.tile([P, T, D1], U8, name="x1_in")
            nc.sync.dma_start(out=x1_in[u][:], in_=group_rows(x1_bytes, u))

        def load_x2(u, parts):
            x2_in[u] = load.tile([P, T, D2], BF16, name="x2_in")
            for h in range(parts):
                k = slice(h * D2 // parts, (h + 1) * D2 // parts)
                nc.sync.dma_start(out=x2_in[u][:, :, k], in_=group_rows(x2, u)[:, :, k])

        def load_scales(tile_rows, rows):
            for q in range(4):
                nc.sync.dma_start(out=tile_rows(slice(32 * q, 32 * q + 4)).bitcast(I32), in_=rows(slice(4 * q, 4 * q + 4)))

        def widen(u, pieces, on_vector):
            if u not in x1_bf:
                x1_bf[u] = work.tile([P, T, D1], BF16, name="x1_bf")
            for piece in pieces:
                t, j = divmod(piece, D1 // K_SCALE)
                cols = slice(K_SCALE * j, K_SCALE * (j + 1))
                dst = x1_bf[u][:, t, cols]
                src = x1_in[u][:, t, cols].bitcast(FP8)
                scale = x1_scale_sb[:, u, t, j : j + 1]
                if on_vector(piece):
                    nc.vector.tensor_scalar(out=dst, in0=src, scalar1=scale, scalar2=None, op0=ALU.mult)
                else:
                    nc.scalar.activation(out=dst, in_=src, func=ACT.Copy, scale=scale)

        def turn(u, operand, last_bank_on_vector=False):
            src, g = (x1_bf[u], 0) if operand == "x1" else (x2_in[u], operand)
            row = src.shape[2] // 2
            words = src[:].rearrange("p t k -> p (t k)").bitcast(F32)
            turned = work.tile([P, PASS, T], BF16, name="x_turned", align_bytes=64)
            turned_words = turned[:].rearrange("p c j -> p (c j)").bitcast(F32)
            for half in range(2):
                bank = x_psum.tile([P, 2, 2, P], F32, name="x_bank")
                for i in range(2):
                    for e in range(2):
                        at = row * (2 * half + i) + PASS // 2 * g + e
                        nc.tensor.transpose(bank[:, i, e, :], words[:, at : at + PASS // 2 - 1 : 2], ident[:])
                dst = turned_words[:, PASS * half : PASS * (half + 1)].rearrange("p (i r e) -> p i r e", i=2, e=2)
                if half == 1 and last_bank_on_vector:
                    nc.vector.tensor_copy(out=dst, in_=bank[:].rearrange("p i e r -> p i r e"))
                else:
                    nc.scalar.copy(out=dst, in_=bank[:].rearrange("p i e r -> p i r e"))
            return turned

        def quantize_x(u, operand, turned):
            codes = code.tile([P, PASS], U32, name="codes_%s" % operand, align_bytes=64)
            scales = code.tile([P, PASS], U8, name="scales_%s" % operand, align_bytes=64)
            nc.vector.quantize_mx(
                out=codes[:].bitcast(FP8X4), scales=scales[:], in_=turned[:].rearrange("p c j -> p (c j)")
            )
            x_codes[u, operand], x_scales[u, operand] = codes, scales

        def multiply(bank, u, operand, t, words, word_scales, start, stop):
            cols = slice(P * t, P * (t + 1))
            nc.tensor.matmul_mx(
                out=bank,
                lhsT=x_codes[u, operand][:, cols].bitcast(FP8X4),
                lhsT_scale=x_scales[u, operand][:, cols],
                rhs=words.bitcast(FP4X4),
                rhs_scale=word_scales,
                start=start,
                stop=stop,
            )

        def project_fm(u, h):
            y[u, h] = work.tile([P, P, T, CHAN], F32, name="y1")
            cols = slice(BANK * h, BANK * (h + 1))
            for t in range(T):
                bank = z_psum.tile([P, BANK], F32, name="z_bank")
                multiply(
                    bank[:], u, "x1", t, w1_sb[:, 2 * BANK * h : 2 * BANK * (h + 1)], w1_scale_sb[:, cols], True, True
                )
                nc.scalar.activation(
                    out=y[u, h][:, :, t, :],
                    in_=bank[:].rearrange("p (c i) -> p c i", i=CHAN),
                    func=ACT.Copy,
                    scale=abs_m[:, u, t : t + 1],
                )

        def project_f2(u):
            y[u, "f2"] = work.tile([P, C2, T], F32, name="y2")
            for j in range(C2 // P):
                cols = slice(P * j, P * (j + 1))
                bank = z_psum.tile([P, T, P], F32, name="z_bank")
                for t in range(T):
                    for g in range(2):
                        words = w2_sb[:, g, 2 * P * j : 2 * P * (j + 1)]
                        multiply(bank[:, t, :], u, g, t, words, w2_scale_sb[:, g, cols], g == 0, g == 1)
                nc.scalar.copy(out=y[u, "f2"][:, cols, :], in_=bank[:].rearrange("p t n -> p n t"))

        def leaky(u, part):
            f[u, part] = work.tile([P, BANK, T], BF16, name="f", align_bytes=64)
            if part == "f2":
                src, dst = y[u, part][:], f[u, part][:]
            else:
                src = y[u, part][:].rearrange("p c t i -> p (c t) i")
                dst = f[u, part][:].rearrange("p (i c) t -> p (c t) i", i=CHAN)
            nc.vector.scalar_tensor_tensor(out=dst, in0=src, scalar=SLOPE, in1=src, op0=ALU.mult, op1=ALU.max)

        def apply_sign(u):
            signed = work.tile([P, C2, T], BF16, name="f2_signed", align_bytes=64)
            signs = sign_m[:, u, :].unsqueeze(1).to_broadcast([P, C2, T])
            nc.vector.tensor_tensor(out=signed[:], in0=f[u, "f2"][:], in1=signs, op=ALU.mult)
            f[u, "f2"] = signed

        def quantize_f(u, part):
            b, g = divmod(u, GROUPS_B)
            if part == "f2":
                codes, scales = f2_codes[:, b, g, :], f2_scales[:, b, g, :]
            else:
                cols = slice(BANK * part, BANK * (part + 1))
                codes, scales = fm_codes[:, b, g, cols], fm_scales[:, b, g, cols]
            nc.vector.quantize_mx(
                out=codes.bitcast(FP8X4), scales=scales, in_=f[u, part][:].rearrange("p n t -> p (n t)")
            )

        def gram_pair(b, pair):
            h, i0 = divmod(2 * pair, CHAN)
            result[b, pair] = work.tile([P, 2, C2], F32, name="result")
            for i in range(2):
                bank = gram_psum.tile([P, C2], F32, name="gram_bank")
                cols = slice(P * (2 * pair + i), P * (2 * pair + i + 1))
                for g in range(GROUPS_B):
                    nc.tensor.matmul_mx(
                        out=bank[:],
                        lhsT=fm_codes[:, b, g, cols].bitcast(FP8X4),
                        lhsT_scale=fm_scales[:, b, g, cols],
                        rhs=f2_codes[:, b, g, :].bitcast(FP8X4),
                        rhs_scale=f2_scales[:, b, g, :],
                        start=(g == 0),
                        stop=(g == GROUPS_B - 1),
                    )
                nc.vector.scalar_tensor_tensor(
                    out=result[b, pair][:, i, :],
                    in0=bank[:],
                    scalar=1.0 / 32.0,
                    in1=a_sb[:, b, h, i0 + i, :],
                    op0=ALU.mult,
                    op1=ALU.subtract,
                )

        def finish_pair(b, pair, blocks):
            h, i0 = divmod(2 * pair, CHAN)
            rows = out[b, BANK * h : BANK * (h + 1)].rearrange("(c i) n -> c i n", i=CHAN)
            for i in range(0, 2, blocks):
                block = result[b, pair][:, i : i + blocks]
                nc.scalar.activation(out=block, in_=block, func=ACT.Tanh)
                nc.sync.dma_start(out=rows[:, i0 + i : i0 + i + blocks], in_=block)

        ctx.enter_context(tc.manual_schedule())

        nc.vector.memset(zero[:], 0.0)
        nc.vector.memset(w1_scale_sb[:].bitcast(I32), 0)
        nc.vector.memset(w2_scale_sb[:].rearrange("p g n -> p (g n)").bitcast(I32), 0)
        make_identity(nc, ident[:])
        load_x1(0)
        nc.sync.dma_start(
            out=x1_scale_sb[:].rearrange("p u t j -> p u (t j)"),
            in_=x1_scale.rearrange("b (g p t) j -> p (b g) (t j)", g=GROUPS_B, t=T),
        )
        load_x2(0, 2)
        nc.sync.dma_start(out=m_sb[:], in_=m.rearrange("b (g p t) -> p (b g) t", g=GROUPS_B, t=T))
        load_scales(lambda p: w1_scale_sb[p, :], lambda r: w1_scales[0, r, :].bitcast(I32))
        nc.sync.dma_start(out=w1_sb[:].bitcast(I32), in_=w1_words[0].bitcast(I32))
        load_x1(1)
        load_scales(lambda p: w2_scale_sb[p, :, :], lambda r: w2_scales[:, r, :].rearrange("g r n -> r g n").bitcast(I32))
        nc.sync.dma_start(out=w2_sb[:].bitcast(I32), in_=w2_words.rearrange("g p n -> p g n").bitcast(I32))
        load_x2(1, 1)
        for u in range(2, GROUPS):
            load_x1(u)
            load_x2(u, 1)
        for b in range(B):
            nc.sync.dma_start(out=a_sb[:, b], in_=a[b].rearrange("(h c i) n -> c h i n", c=P, i=CHAN))
        nc.scalar.activation(out=tanh_zero[:], in_=zero[:], func=ACT.Tanh)
        nc.gpsimd.tensor_scalar(out=twice_positive[:], in0=m_sb[:], scalar1=tanh_zero[:], scalar2=2.0, op0=ALU.is_ge, op1=ALU.mult)
        nc.gpsimd.tensor_scalar(out=sign_m[:], in0=twice_positive[:], scalar1=1.0, scalar2=0.0, op0=ALU.subtract, op1=ALU.add)
        nc.gpsimd.tensor_tensor(out=abs_m[:], in0=m_sb[:], in1=sign_m[:], op=ALU.mult)

        steps, to_turn = [], []
        for u in range(GROUPS):
            f2_first = u == GROUPS - 1
            steps += [(u, "f2"), (u, 0), (u, 1)] if f2_first else [(u, 0), (u, 1), (u, "f2")]
            to_turn += [(u, 0), (u, 1), (u, "x1")] if f2_first else [(u, "x1"), (u, 0), (u, 1)]
        two_turns_step = 5
        widen_in_step = {0: (1, range(1, PIECES, 2))}
        for third in range(3):
            widen_in_step[1 + third] = (2, range(third, PIECES, 3))
            widen_in_step[5 + third] = (3, range(third, PIECES, 3))
        pairs = C1 // P // 2
        pair_in_step = {7 + pair: (0, pair) for pair in range(pairs)}
        pair_in_step[len(steps) - 1] = (1, 0)

        widen(0, range(PIECES), lambda n: n * VECTOR_PIECES // PIECES != (n + 1) * VECTOR_PIECES // PIECES)
        for operand in to_turn[:2]:
            quantize_x(*operand, turn(*operand, last_bank_on_vector=True))
        widen(1, range(0, PIECES, 2), lambda n: True)
        n_turned = 2

        turned = []
        for k, (u, part) in enumerate(steps):
            for operand, tile in turned:
                quantize_x(*operand, tile)
            signed = steps[k - 1] if k > 0 and steps[k - 1][1] == "f2" else None
            if signed:
                apply_sign(signed[0])
            elif k > 0:
                quantize_f(*steps[k - 1])

            if part == "f2":
                project_f2(u)
            else:
                project_fm(u, part)
            if k - 1 in pair_in_step:
                finish_pair(*pair_in_step[k - 1], 2)
            if k in pair_in_step:
                gram_pair(*pair_in_step[k])

            first, n_turned = n_turned, n_turned + (2 if k == two_turns_step else 1)
            turned = [(operand, turn(*operand)) for operand in to_turn[first:n_turned]]
            if k in widen_in_step:
                widen(*widen_in_step[k], lambda n, group=widen_in_step[k][0]: group == 1)
            leaky(u, part)
            if signed:
                quantize_f(*signed)

        quantize_f(*steps[-1])
        finish_pair(1, 0, 2)
        for pair in range(1, pairs):
            gram_pair(1, pair)
            finish_pair(1, pair, 1)
